import numpy as np
import ml_dtypes


def mxq(x, axis, fmt="e4m3"):
    dtype, down = {"e4m3": (ml_dtypes.float8_e4m3fn, 7), "e5m2": (ml_dtypes.float8_e5m2, 14)}[fmt]
    v = np.moveaxis(np.asarray(x, np.float32).astype(ml_dtypes.bfloat16).astype(np.float64), axis, -1)
    blocks = v.reshape(v.shape[:-1] + (-1, 32))
    amax = np.abs(blocks).max(-1, keepdims=True)
    byte = np.maximum(np.where(amax > 0, np.frexp(amax)[1] - 1 + 127, 0) - down, 1)
    scale = np.exp2(byte - 127.0)
    codes = (blocks / scale).astype(np.float32).astype(dtype).astype(np.float64)
    return np.moveaxis((codes * scale).reshape(v.shape), -1, axis)


WIDE = False


def mx_kscale(k):
    if not WIDE:
        return np.ones(k)
    levels = np.array([10, -10, 5, -5, 0])
    if k % 512:
        return np.exp2(np.random.permutation(np.resize(levels, k // 32))).repeat(32)
    a = np.empty((k // 512, 16))
    for p in range(k // 512):
        a[p, :8] = np.random.permutation(np.resize(levels, 8))
        for g in range(8):
            far = levels[np.abs(levels - a[p, g]) >= 10]
            a[p, g + 8] = far[np.random.randint(len(far))]
    return np.exp2(a.ravel()).repeat(32)


def f64(x):
    return np.asarray(x).astype(np.float64)


def striped(idx):
    return np.tile(np.asarray(idx).reshape(-1, 16).T, (8, 1)).astype(np.uint16)


def unstriped(offs):
    return offs[:16].T.reshape(-1).astype(np.int64)


E2M1 = np.array([0.0, 0.5, 1.0, 1.5, 2.0, 3.0, 4.0, 6.0, -0.0, -0.5, -1.0, -1.5, -2.0, -3.0, -4.0, -6.0])


def pack_weight(w, fmt):
    k, n = w.shape
    w = f64(np.asarray(w, np.float32).astype(ml_dtypes.bfloat16)).reshape(k // 32, 32, n)
    amax = np.abs(w).max(1)
    if fmt == "e4m3":
        byte = np.frexp(amax)[1] - 1 + 127 - 7
    else:
        mant, ex = np.frexp(amax / 6.0)
        byte = np.where(mant > 0.5, ex, ex - 1) + 127
    byte = np.clip(np.where(amax > 0, byte, 1), 1, 254)
    scaled = (w * np.exp2(127.0 - byte)[:, None, :]).reshape(k, n).astype(np.float32)
    by_word = np.ascontiguousarray(scaled.reshape(k // 512, 128, 4, n).transpose(0, 1, 3, 2))
    if fmt == "e4m3":
        words = by_word.astype(ml_dtypes.float8_e4m3fn).view(np.uint8)
    else:
        c = by_word.astype(ml_dtypes.float4_e2m1fn).view(np.uint8) & 0xF
        words = (c[..., 0::2] | (c[..., 1::2] << 4)).reshape(k // 512, 128, 2 * n)
    return np.ascontiguousarray(words), np.ascontiguousarray(byte.astype(np.uint8).reshape(k // 512, 16, n))


def unpack_weight(words, scales, fmt):
    g, _, n = scales.shape
    words = np.ascontiguousarray(words).reshape(g, 128, n, -1)
    if fmt == "e4m3":
        vals = words.view(ml_dtypes.float8_e4m3fn).astype(np.float64)
    else:
        nib = np.empty((g, 128, n, 4), np.uint8)
        nib[..., 0::2] = words & 0xF
        nib[..., 1::2] = words >> 4
        vals = E2M1[nib]
    vals = vals * np.repeat(np.exp2(scales.astype(np.float64) - 127.0), 8, axis=1)[..., None]
    return vals.transpose(0, 1, 3, 2).reshape(g * 512, n)


K, T, J, R, N = 512, 1024, 512, 512, 512


def setup_inputs():
    n = np.random.standard_normal
    idx = np.random.permutation(T)[:J]
    fk = mx_kscale(K)
    fr = mx_kscale(R)
    xtp = pack_weight(n((K, T)) / fk[:, None], "e4m3")
    wap = pack_weight(n((K, R)) * 1 / np.sqrt(K) * fk[:, None] * fr, "e2m1")
    wbp = pack_weight(n((R, N)) * 1 / np.sqrt(R) / fr[:, None], "e4m3")
    return {
        "xt_words": xtp[0],
        "xt_scales": xtp[1],
        "wa_words": wap[0],
        "wa_scales": wap[1],
        "dc": (np.random.uniform(0.3, 0.9, (R, 1))).astype(np.float32),
        "wb_words": wbp[0],
        "wb_scales": wbp[1],
        "ga": (np.random.uniform(0.4, 1.2, (1, J))).astype(np.float32),
        "offs": striped(idx),
    }


def reference(xt_words, xt_scales, wa_words, wa_scales, dc, wb_words, wb_scales, ga, offs):
    idx = unstriped(offs)
    xtu = unpack_weight(xt_words, xt_scales, "e4m3")
    wau = unpack_weight(wa_words, wa_scales, "e2m1")
    wbu = unpack_weight(wb_words, wb_scales, "e4m3")
    xtidxg = xtu[:, idx]
    a = wau.T @ xtidxg
    h1 = np.maximum(a, 0.0)
    hp = np.pad(h1, ((0, 0), (1, 0)))[:, :J]
    hid = h1 + f64(dc) * hp
    hidq = mxq(hid, 0, "e4m3")
    p = wbu.T @ hidq
    pw = p * f64(ga)
    y = np.zeros((N, T))
    y[:, idx] = pw
    return y

@@ -1,0 +1,228 @@
+from contextlib import ExitStack
+
+import concourse.mybir as mybir
+from concourse.masks import make_identity
+
+K, T, J, R, N = 512, 1024, 512, 512, 512
+FLOPS = 2 * K * R * J + 2 * R * N * J
+
+F32 = mybir.dt.float32
+BF16 = mybir.dt.bfloat16
+I32 = mybir.dt.int32
+U32 = mybir.dt.uint32
+U16 = mybir.dt.uint16
+U8 = mybir.dt.uint8
+FP8X4 = mybir.dt.float8_e4m3fn_x4
+FP4X4 = mybir.dt.float4_e2m1fn_x4
+MULT = mybir.AluOpType.mult
+ADD = mybir.AluOpType.add
+RELU = mybir.ActivationFunctionType.Relu
+
+P = 128
+PACK = 4
+BANK = 512
+PAD = 8
+CHUNKS = (128, 384)
+
+
+def load_scale_rows(queue, plane, scales, rows):
+    src = scales[0].rearrange("(q i) c -> i q c", i=4)
+    for i in rows:
+        queue.dma_start(out=plane[i:P:32, :].bitcast(I32), in_=src[i].bitcast(I32))
+
+
+def pieces(width):
+    out, start = [], 0
+    while start < width:
+        w = 512 if width - start >= 512 else (256 if width - start >= 256 else 128)
+        out.append((start, w))
+        start = start + w
+    return out
+
+
+def tile_moe_expert_hidden_taps_scattered_kernel(
+    tc, xt_words, xt_scales, wa_words, wa_scales, dc, wb_words, wb_scales, ga, offs, out
+):
+    nc = tc.nc
+    with ExitStack() as ctx:
+        keep = ctx.enter_context(tc.tile_pool(name="keep", bufs=1))
+        psum = ctx.enter_context(tc.psum_pool(name="psum", bufs=1))
+
+        offsets = keep.tile([P, J // 16], U16, name="offsets")
+        x_words = keep.tile([P, T], I32, name="x_words", align_bytes=64)
+        x_plane = keep.tile([P, T], U8, name="x_plane", align_bytes=64)
+        wa_raw = keep.tile([P, 2 * R], U8, name="wa_raw", align_bytes=64)
+        wa_raw_plane = keep.tile([P, R], U8, name="wa_raw_plane", align_bytes=64)
+        wa_codes = keep.tile([P, 2 * R], U8, name="wa_codes", align_bytes=64)
+        wa_plane = keep.tile([P, R], U8, name="wa_plane", align_bytes=64)
+        wb_codes = keep.tile([P, N], I32, name="wb_codes", align_bytes=64)
+        wb_plane = keep.tile([P, N], U8, name="wb_plane", align_bytes=64)
+        dc_sb = keep.tile([P, PACK], F32, name="dc_sb")
+        ga_rows = keep.tile([P, PACK], F32, name="ga_rows")
+        ident = keep.tile([P, P], F32, name="ident")
+        ga_sb = keep.tile([P, J], F32, name="ga_sb")
+        h1 = keep.tile([P, PACK, PAD + J], F32, name="h1", align_bytes=64)
+        zeros = keep.tile([P, PACK, PAD], F32, name="zeros")
+        windows = [keep.tile([P, T], F32, name="window%d" % b) for b in range(N // P)]
+
+        nc.vector.memset(wa_raw_plane[:].bitcast(I32), 0)
+        nc.vector.memset(x_plane[:].bitcast(I32), 0)
+        nc.vector.memset(wb_plane[:].bitcast(I32), 0)
+        nc.vector.memset(zeros[:], 0.0)
+
+        nc.sync.dma_start(offsets[:], offs)
+        load_scale_rows(nc.scalar, wa_raw_plane, wa_scales, range(4))
+        nc.sync.dma_start(out=wa_raw[:].bitcast(I32), in_=wa_words[0].bitcast(I32))
+        nc.sync.dma_start(out=x_words[:], in_=xt_words[0].rearrange("p n t -> p (n t)").bitcast(I32))
+        load_scale_rows(nc.sync, x_plane, xt_scales, range(4))
+        nc.gpsimd.dma_start(out=ga_rows[:], in_=ga.rearrange("o (p m) -> p (o m)", m=PACK))
+        make_identity(nc, ident[:])
+        nc.gpsimd.dma_start(out=dc_sb[:], in_=dc.rearrange("(p t) o -> p (t o)", t=PACK))
+        nc.sync.dma_start(out=wb_codes[:], in_=wb_words[0].rearrange("p n t -> p (n t)").bitcast(I32))
+        load_scale_rows(nc.sync, wb_plane, wb_scales, range(4))
+        nc.scalar.activation(h1[:, :, 0:PAD], zeros[:], RELU)
+
+        for b in range(N // P):
+            eng = nc.vector if b < 4 else nc.gpsimd
+            eng.memset(windows[b][:].bitcast(I32), 0)
+
+        nc.vector.tensor_copy(
+            wa_codes[:].bitcast(U16).rearrange("p (t m) -> p t m", t=PACK),
+            wa_raw[:].bitcast(U16).rearrange("p (m t) -> p t m", t=PACK),
+        )
+        nc.vector.tensor_copy(
+            wa_plane[:].rearrange("p (t m) -> p t m", t=PACK),
+            wa_raw_plane[:].rearrange("p (m t) -> p t m", t=PACK),
+        )
+
+        starts = [sum(CHUNKS[:c]) for c in range(len(CHUNKS))]
+        state = {"turn": 0}
+
+        def banks_for(width, per, tags):
+            views, groups = [], []
+            for g in range(PACK // per):
+                bank = psum.tile([P, BANK], F32, name="bank", tag="bank%d" % tags[g])
+                v = bank[:, 0 : per * width].rearrange("p (t j) -> p t j", t=per)
+                groups.append((v, g * per, per))
+                views.extend(v[:, i, :] for i in range(per))
+            return views, groups
+
+        def spread_ga():
+            views, groups = banks_for(P, PACK, [7])
+            for m in range(PACK):
+                nc.tensor.transpose(views[m], ga_rows[:, m : m + 1].to_broadcast([P, P]), ident[:])
+            nc.scalar.copy(ga_sb[:].rearrange("p (n m) -> p n m", m=PACK), groups[0][0].rearrange("p m n -> p n m"))
+
+        def gather(c):
+            j0, w = starts[c], CHUNKS[c]
+            lst = offsets[:, j0 // 16 : (j0 + w) // 16]
+            words = keep.tile([P, w], U32, name="xg_words%d" % c, align_bytes=64)
+            plane = keep.tile([P, w], U8, name="xg_plane%d" % c, align_bytes=64)
+            nc.vector.tensor_copy(words[:], x_words[:].bitcast(U32).indirect(lst))
+            nc.vector.tensor_copy(plane[:], x_plane[:].indirect(lst))
+            state["x", c] = (words, plane)
+
+        def layer1(c, per_bank, tags):
+            j0, w = starts[c], CHUNKS[c]
+            words, plane = state["x", c]
+            views, groups = banks_for(w, per_bank, tags)
+            for v, t0, per in groups:
+                for t in range(t0, t0 + per):
+                    for s, n in pieces(w):
+                        nc.tensor.matmul_mx(
+                            out=views[t][:, s : s + n],
+                            lhsT=wa_codes[:, 2 * P * t : 2 * P * (t + 1)].bitcast(FP4X4),
+                            lhsT_scale=wa_plane[:, P * t : P * (t + 1)],
+                            rhs=words[:, s : s + n].bitcast(FP8X4),
+                            rhs_scale=plane[:, s : s + n],
+                            start=True,
+                            stop=True,
+                        )
+                nc.scalar.activation(h1[:, t0 : t0 + per, PAD + j0 : PAD + j0 + w], v, RELU)
+
+        def taps(c):
+            j0, w = starts[c], CHUNKS[c]
+            hid = keep.tile([P, PACK, w], BF16, name="hid%d" % c, tag="hid%d" % c, align_bytes=64)
+            for t in range(PACK):
+                nc.vector.scalar_tensor_tensor(
+                    hid[:, t, :],
+                    h1[:, t, PAD + j0 - 1 : PAD + j0 - 1 + w],
+                    dc_sb[:, t : t + 1],
+                    h1[:, t, PAD + j0 : PAD + j0 + w],
+                    MULT,
+                    ADD,
+                )
+            state["hid", c] = hid
+
+        def weave(c, on_vector):
+            w = CHUNKS[c]
+            grouped = keep.tile([P, w, PACK], BF16, name="grouped%d" % c, align_bytes=64)
+            src = state["hid", c][:].rearrange("p t (c i) -> p c t i", i=4)
+            dst = grouped[:].rearrange("p (c i) t -> p c t i", i=4)
+            if on_vector:
+                nc.vector.tensor_copy(dst, src)
+            else:
+                nc.scalar.copy(dst, src)
+            state["grouped", c] = grouped
+
+        def quantise(c):
+            w = CHUNKS[c]
+            codes = keep.tile([P, w], U32, name="h_codes%d" % c, align_bytes=64)
+            plane = keep.tile([P, w], U8, name="h_plane%d" % c, align_bytes=64)
+            flat = state["grouped", c][:].rearrange("p j t -> p (j t)")
+            for s, n in pieces(w):
+                nc.vector.quantize_mx(
+                    out=codes[:, s : s + n].bitcast(FP8X4),
+                    scales=plane[:, s : s + n],
+                    in_=flat[:, PACK * s : PACK * (s + n)],
+                )
+            state["h", c] = (codes, plane)
+
+        def layer2(c, per_bank, tags, held):
+            w = CHUNKS[c]
+            codes, plane = state["h", c]
+            views, groups = banks_for(w, per_bank, tags)
+            res = []
+            for v, b0, per in groups:
+                for b in range(b0, b0 + per):
+                    for s, n in pieces(w):
+                        nc.tensor.matmul_mx(
+                            out=views[b][:, s : s + n],
+                            lhsT=wb_codes[:, P * b : P * (b + 1)].bitcast(FP8X4),
+                            lhsT_scale=wb_plane[:, P * b : P * (b + 1)],
+                            rhs=codes[:, s : s + n].bitcast(FP8X4),
+                            rhs_scale=plane[:, s : s + n],
+                            start=True,
+                            stop=True,
+                        )
+                p_sb = keep.tile([P, per, w], F32, name="p%d_%d" % (c, b0), tag=held.get(b0, "p%d_%d" % (c, b0)), align_bytes=64)
+                nc.scalar.copy(p_sb[:], v)
+                res.extend(p_sb[:, i, :] for i in range(per))
+            state["p", c] = res
+
+        def scatter(c, blocks):
+            j0, w = starts[c], CHUNKS[c]
+            lst = offsets[:, j0 // 16 : (j0 + w) // 16]
+            for b in blocks:
+                nc.vector.tensor_tensor(
+                    windows[b][:].indirect(lst), state["p", c][b], ga_sb[:, j0 : j0 + w], MULT
+                )
+                if c == len(CHUNKS) - 1:
+                    nc.sync.dma_start(out=out[P * b : P * (b + 1), :], in_=windows[b][:])
+
+        spread_ga()
+        gather(0)
+        layer1(0, 1, [0, 1, 2, 3])
+        gather(1)
+        taps(0)
+        weave(0, True)
+        layer1(1, 1, [4, 5, 6, 7])
+        quantise(0)
+        taps(1)
+        weave(1, False)
+        layer2(0, 2, [0, 1], {2: "hid1"})
+        scatter(0, [0, 1])
+        quantise(1)
+        layer2(1, 1, [2, 3, 4, 5], {})
+        scatter(0, [2, 3])
+        scatter(1, range(4))

@@ -51,38 +51,36 @@ def tile_moe_expert_hidden_taps_scattered_kernel(
         offsets = keep.tile([P, J // 16], U16, name="offsets")
         x_words = keep.tile([P, T], I32, name="x_words", align_bytes=64)
         x_plane = keep.tile([P, T], U8, name="x_plane", align_bytes=64)
-        wa_raw = keep.tile([P, 2 * R], U8, name="wa_raw", align_bytes=64)
-        wa_raw_plane = keep.tile([P, R], U8, name="wa_raw_plane", align_bytes=64)
+        wa_raw = keep.tile([P, 2 * R], U8, name="wa_raw", tag="raw_words", align_bytes=64)
+        wa_raw_plane = keep.tile([P, R], U8, name="wa_raw_plane", tag="raw_plane", align_bytes=64)
         wa_codes = keep.tile([P, 2 * R], U8, name="wa_codes", align_bytes=64)
         wa_plane = keep.tile([P, R], U8, name="wa_plane", align_bytes=64)
-        wb_codes = keep.tile([P, N], I32, name="wb_codes", align_bytes=64)
         wb_plane = keep.tile([P, N], U8, name="wb_plane", align_bytes=64)
-        dc_sb = keep.tile([P, PACK], F32, name="dc_sb")
-        ga_rows = keep.tile([P, PACK], F32, name="ga_rows")
         ident = keep.tile([P, P], F32, name="ident")
         ga_sb = keep.tile([P, J], F32, name="ga_sb")
-        h1 = keep.tile([P, PACK, PAD + J], F32, name="h1", align_bytes=64)
-        zeros = keep.tile([P, PACK, PAD], F32, name="zeros")
-        windows = [keep.tile([P, T], F32, name="window%d" % b) for b in range(N // P)]
+        h1 = [keep.tile([P, PAD + J], F32, name="h1_%d" % t, tag="h1_%d" % t, align_bytes=64) for t in range(PACK)]
+        zeros = keep.tile([P, PAD], F32, name="zeros", tag="small")
+        windows = [keep.tile([P, T], F32, name="window%d" % b) for b in range(2)]
 
         nc.vector.memset(wa_raw_plane[:].bitcast(I32), 0)
-        nc.vector.memset(x_plane[:].bitcast(I32), 0)
+        nc.gpsimd.memset(x_plane[:].bitcast(I32), 0)
         nc.vector.memset(wb_plane[:].bitcast(I32), 0)
         nc.vector.memset(zeros[:], 0.0)
 
         nc.sync.dma_start(offsets[:], offs)
-        load_scale_rows(nc.scalar, wa_raw_plane, wa_scales, range(4))
         nc.sync.dma_start(out=wa_raw[:].bitcast(I32), in_=wa_words[0].bitcast(I32))
         nc.sync.dma_start(out=x_words[:], in_=xt_words[0].rearrange("p n t -> p (n t)").bitcast(I32))
-        load_scale_rows(nc.sync, x_plane, xt_scales, range(4))
-        nc.gpsimd.dma_start(out=ga_rows[:], in_=ga.rearrange("o (p m) -> p (o m)", m=PACK))
-        make_identity(nc, ident[:])
-        nc.gpsimd.dma_start(out=dc_sb[:], in_=dc.rearrange("(p t) o -> p (t o)", t=PACK))
-        nc.sync.dma_start(out=wb_codes[:], in_=wb_words[0].rearrange("p n t -> p (n t)").bitcast(I32))
+        load_scale_rows(nc.scalar, wa_raw_plane, wa_scales, range(4))
+        load_scale_rows(nc.gpsimd, x_plane, xt_scales, [3])
+        load_scale_rows(nc.sync, x_plane, xt_scales, range(3))
         load_scale_rows(nc.sync, wb_plane, wb_scales, range(4))
-        nc.scalar.activation(h1[:, :, 0:PAD], zeros[:], RELU)
+        for t in range(PACK):
+            nc.scalar.activation(h1[t][:, 0:PAD], zeros[:], RELU)
+        dc_sb = keep.tile([P, PACK], F32, name="dc_sb", tag="small")
+        nc.sync.dma_start(out=dc_sb[:], in_=dc.rearrange("(p t) o -> p (t o)", t=PACK))
+        make_identity(nc, ident[:])
 
-        for b in range(N // P):
+        for b in range(2):
             eng = nc.vector if b < 4 else nc.gpsimd
             eng.memset(windows[b][:].bitcast(I32), 0)
 
@@ -94,6 +92,11 @@ def tile_moe_expert_hidden_taps_scattered_kernel(
             wa_plane[:].rearrange("p (t m) -> p t m", t=PACK),
             wa_raw_plane[:].rearrange("p (m t) -> p t m", t=PACK),
         )
+
+        wb_codes = keep.tile([P, N], I32, name="wb_codes", tag="raw_words", align_bytes=64)
+        nc.sync.dma_start(out=wb_codes[:], in_=wb_words[0].rearrange("p n t -> p (n t)").bitcast(I32))
+        ga_rows = keep.tile([P, PACK], F32, name="ga_rows", tag="raw_plane", align_bytes=64)
+        nc.sync.dma_start(out=ga_rows[:], in_=ga.rearrange("o (p m) -> p (o m)", m=PACK))
 
         starts = [sum(CHUNKS[:c]) for c in range(len(CHUNKS))]
         state = {"turn": 0}
@@ -107,11 +110,16 @@ def tile_moe_expert_hidden_taps_scattered_kernel(
                 views.extend(v[:, i, :] for i in range(per))
             return views, groups
 
-        def spread_ga():
-            views, groups = banks_for(P, PACK, [7])
+        def spread_ga(bank_tag):
+            views, groups = banks_for(P, PACK, [bank_tag])
             for m in range(PACK):
                 nc.tensor.transpose(views[m], ga_rows[:, m : m + 1].to_broadcast([P, P]), ident[:])
             nc.scalar.copy(ga_sb[:].rearrange("p (n m) -> p n m", m=PACK), groups[0][0].rearrange("p m n -> p n m"))
+
+        def late_window(b, tag):
+            win = keep.tile([P, T], F32, name="window%d" % b, tag=tag, align_bytes=64)
+            nc.gpsimd.memset(win[:].bitcast(I32), 0)
+            windows.append(win)
 
         def gather(c):
             j0, w = starts[c], CHUNKS[c]
@@ -138,7 +146,7 @@ def tile_moe_expert_hidden_taps_scattered_kernel(
                             start=True,
                             stop=True,
                         )
-                nc.scalar.activation(h1[:, t0 : t0 + per, PAD + j0 : PAD + j0 + w], v, RELU)
+                nc.scalar.activation(h1[t0][:, PAD + j0 : PAD + j0 + w], views[t0], RELU)
 
         def taps(c):
             j0, w = starts[c], CHUNKS[c]
@@ -146,28 +154,29 @@ def tile_moe_expert_hidden_taps_scattered_kernel(
             for t in range(PACK):
                 nc.vector.scalar_tensor_tensor(
                     hid[:, t, :],
-                    h1[:, t, PAD + j0 - 1 : PAD + j0 - 1 + w],
+                    h1[t][:, PAD + j0 - 1 : PAD + j0 - 1 + w],
                     dc_sb[:, t : t + 1],
-                    h1[:, t, PAD + j0 : PAD + j0 + w],
+                    h1[t][:, PAD + j0 : PAD + j0 + w],
                     MULT,
                     ADD,
                 )
             state["hid", c] = hid
 
-        def weave(c, on_vector):
+        def weave(c, on_vector, tag):
             w = CHUNKS[c]
-            grouped = keep.tile([P, w, PACK], BF16, name="grouped%d" % c, align_bytes=64)
-            src = state["hid", c][:].rearrange("p t (c i) -> p c t i", i=4)
-            dst = grouped[:].rearrange("p (c i) t -> p c t i", i=4)
-            if on_vector:
-                nc.vector.tensor_copy(dst, src)
-            else:
-                nc.scalar.copy(dst, src)
+            grouped = keep.tile([P, w, PACK], BF16, name="grouped%d" % c, tag=tag, align_bytes=64)
+            for s, n in pieces(w):
+                src = state["hid", c][:, :, s : s + n].rearrange("p t (c i) -> p c t i", i=4)
+                dst = grouped[:, s : s + n, :].rearrange("p (c i) t -> p c t i", i=4)
+                if on_vector:
+                    nc.vector.tensor_copy(dst, src)
+                else:
+                    nc.scalar.copy(dst, src)
             state["grouped", c] = grouped
 
         def quantise(c):
             w = CHUNKS[c]
-            codes = keep.tile([P, w], U32, name="h_codes%d" % c, align_bytes=64)
+            codes = keep.tile([P, w], U32, name="h_codes%d" % c, tag="h_codes%d" % c, align_bytes=64)
             plane = keep.tile([P, w], U8, name="h_plane%d" % c, align_bytes=64)
             flat = state["grouped", c][:].rearrange("p j t -> p (j t)")
             for s, n in pieces(w):
@@ -178,11 +187,11 @@ def tile_moe_expert_hidden_taps_scattered_kernel(
                 )
             state["h", c] = (codes, plane)
 
-        def layer2(c, per_bank, tags, held):
+        def layer2(c, per_bank, tags):
             w = CHUNKS[c]
             codes, plane = state["h", c]
             views, groups = banks_for(w, per_bank, tags)
-            res = []
+            state["acc", c] = groups
             for v, b0, per in groups:
                 for b in range(b0, b0 + per):
                     for s, n in pieces(w):
@@ -195,34 +204,43 @@ def tile_moe_expert_hidden_taps_scattered_kernel(
                             start=True,
                             stop=True,
                         )
-                p_sb = keep.tile([P, per, w], F32, name="p%d_%d" % (c, b0), tag=held.get(b0, "p%d_%d" % (c, b0)), align_bytes=64)
-                nc.scalar.copy(p_sb[:], v)
-                res.extend(p_sb[:, i, :] for i in range(per))
-            state["p", c] = res
+
+        def drain(c, g, tag):
+            v, b0, per = state["acc", c][g]
+            p_sb = keep.tile([P, per, CHUNKS[c]], F32, name="p%d_%d" % (c, b0), tag=tag, align_bytes=64)
+            nc.scalar.copy(p_sb[:], v)
+            for i in range(per):
+                state["p", c, b0 + i] = p_sb[:, i, :]
 
         def scatter(c, blocks):
             j0, w = starts[c], CHUNKS[c]
             lst = offsets[:, j0 // 16 : (j0 + w) // 16]
             for b in blocks:
                 nc.vector.tensor_tensor(
-                    windows[b][:].indirect(lst), state["p", c][b], ga_sb[:, j0 : j0 + w], MULT
+                    windows[b][:].indirect(lst), state["p", c, b], ga_sb[:, j0 : j0 + w], MULT
                 )
                 if c == len(CHUNKS) - 1:
                     nc.sync.dma_start(out=out[P * b : P * (b + 1), :], in_=windows[b][:])
 
-        spread_ga()
         gather(0)
         layer1(0, 1, [0, 1, 2, 3])
         gather(1)
         taps(0)
-        weave(0, True)
+        weave(0, True, "grouped0")
         layer1(1, 1, [4, 5, 6, 7])
+        spread_ga(2)
         quantise(0)
+        late_window(2, "grouped0")
         taps(1)
-        weave(1, False)
-        layer2(0, 2, [0, 1], {2: "hid1"})
+        late_window(3, "h1_1")
+        layer2(0, 2, [0, 1])
+        drain(0, 0, "h1_2")
+        weave(1, False, "h_codes0")
+        drain(0, 1, "hid1")
         scatter(0, [0, 1])
         quantise(1)
-        layer2(1, 1, [2, 3, 4, 5], {})
+        layer2(1, 1, [2, 3, 4, 5])
+        for g in range(4):
+            drain(1, g, "p1_%d" % g)
         scatter(0, [2, 3])
         scatter(1, range(4))

@@ -71,8 +71,7 @@ def tile_moe_expert_hidden_taps_scattered_kernel(
         nc.sync.dma_start(out=wa_raw[:].bitcast(I32), in_=wa_words[0].bitcast(I32))
         nc.sync.dma_start(out=x_words[:], in_=xt_words[0].rearrange("p n t -> p (n t)").bitcast(I32))
         load_scale_rows(nc.scalar, wa_raw_plane, wa_scales, range(4))
-        load_scale_rows(nc.gpsimd, x_plane, xt_scales, [3])
-        load_scale_rows(nc.sync, x_plane, xt_scales, range(3))
+        load_scale_rows(nc.sync, x_plane, xt_scales, range(4))
         load_scale_rows(nc.sync, wb_plane, wb_scales, range(4))
         for t in range(PACK):
             nc.scalar.activation(h1[t][:, 0:PAD], zeros[:], RELU)
@@ -150,7 +149,7 @@ def tile_moe_expert_hidden_taps_scattered_kernel(
 
         def taps(c):
             j0, w = starts[c], CHUNKS[c]
-            hid = keep.tile([P, PACK, w], BF16, name="hid%d" % c, tag="hid%d" % c, align_bytes=64)
+            hid = keep.tile([P, PACK, w], BF16, name="hid%d" % c, tag="hid1", align_bytes=64)
             for t in range(PACK):
                 nc.vector.scalar_tensor_tensor(
                     hid[:, t, :],
@@ -219,8 +218,12 @@ def tile_moe_expert_hidden_taps_scattered_kernel(
                 nc.vector.tensor_tensor(
                     windows[b][:].indirect(lst), state["p", c, b], ga_sb[:, j0 : j0 + w], MULT
                 )
-                if c == len(CHUNKS) - 1:
+                if c == len(CHUNKS) - 1 and b < 3:
                     nc.sync.dma_start(out=out[P * b : P * (b + 1), :], in_=windows[b][:])
+                if c == len(CHUNKS) - 1 and b == 3:
+                    half = T // 2
+                    nc.sync.dma_start(out=out[P * b : P * (b + 1), 0:half], in_=windows[b][:, 0:half])
+                    nc.scalar.dma_start(out=out[P * b : P * (b + 1), half:T], in_=windows[b][:, half:T])
 
         gather(0)
         layer1(0, 1, [0, 1, 2, 3])

from contextlib import ExitStack

import concourse.mybir as mybir
from concourse.masks import make_identity

K, T, J, R, N = 512, 1024, 512, 512, 512
FLOPS = 2 * K * R * J + 2 * R * N * J

F32 = mybir.dt.float32
BF16 = mybir.dt.bfloat16
I32 = mybir.dt.int32
U32 = mybir.dt.uint32
U16 = mybir.dt.uint16
U8 = mybir.dt.uint8
FP8X4 = mybir.dt.float8_e4m3fn_x4
FP4X4 = mybir.dt.float4_e2m1fn_x4
MULT = mybir.AluOpType.mult
ADD = mybir.AluOpType.add
RELU = mybir.ActivationFunctionType.Relu

P = 128
PACK = 4
BANK = 512
PAD = 8
CHUNKS = (128, 384)


def load_scale_rows(queue, plane, scales, rows):
    src = scales[0].rearrange("(q i) c -> i q c", i=4)
    for i in rows:
        queue.dma_start(out=plane[i:P:32, :].bitcast(I32), in_=src[i].bitcast(I32))


def pieces(width):
    out, start = [], 0
    while start < width:
        w = 512 if width - start >= 512 else (256 if width - start >= 256 else 128)
        out.append((start, w))
        start = start + w
    return out


def tile_moe_expert_hidden_taps_scattered_kernel(
    tc, xt_words, xt_scales, wa_words, wa_scales, dc, wb_words, wb_scales, ga, offs, out
):
    nc = tc.nc
    with ExitStack() as ctx:
        keep = ctx.enter_context(tc.tile_pool(name="keep", bufs=1))
        psum = ctx.enter_context(tc.psum_pool(name="psum", bufs=1))

        offsets = keep.tile([P, J // 16], U16, name="offsets")
        x_words = keep.tile([P, T], I32, name="x_words", align_bytes=64)
        x_plane = keep.tile([P, T], U8, name="x_plane", align_bytes=64)
        wa_raw = keep.tile([P, 2 * R], U8, name="wa_raw", tag="raw_words", align_bytes=64)
        wa_raw_plane = keep.tile([P, R], U8, name="wa_raw_plane", tag="raw_plane", align_bytes=64)
        wa_codes = keep.tile([P, 2 * R], U8, name="wa_codes", align_bytes=64)
        wa_plane = keep.tile([P, R], U8, name="wa_plane", align_bytes=64)
        wb_plane = keep.tile([P, N], U8, name="wb_plane", align_bytes=64)
        ident = keep.tile([P, P], F32, name="ident")
        ga_sb = keep.tile([P, J], F32, name="ga_sb")
        h1 = [keep.tile([P, PAD + J], F32, name="h1_%d" % t, tag="h1_%d" % t, align_bytes=64) for t in range(PACK)]
        zeros = keep.tile([P, PAD], F32, name="zeros", tag="small")
        windows = [keep.tile([P, T], F32, name="window%d" % b) for b in range(2)]

        nc.vector.memset(wa_raw_plane[:].bitcast(I32), 0)
        nc.gpsimd.memset(x_plane[:].bitcast(I32), 0)
        nc.vector.memset(wb_plane[:].bitcast(I32), 0)
        nc.vector.memset(zeros[:], 0.0)

        nc.sync.dma_start(offsets[:], offs)
        nc.sync.dma_start(out=wa_raw[:].bitcast(I32), in_=wa_words[0].bitcast(I32))
        nc.sync.dma_start(out=x_words[:], in_=xt_words[0].rearrange("p n t -> p (n t)").bitcast(I32))
        load_scale_rows(nc.scalar, wa_raw_plane, wa_scales, range(4))
        load_scale_rows(nc.sync, x_plane, xt_scales, range(4))
        load_scale_rows(nc.sync, wb_plane, wb_scales, range(4))
        for t in range(PACK):
            nc.scalar.activation(h1[t][:, 0:PAD], zeros[:], RELU)
        dc_sb = keep.tile([P, PACK], F32, name="dc_sb", tag="small")
        nc.sync.dma_start(out=dc_sb[:], in_=dc.rearrange("(p t) o -> p (t o)", t=PACK))
        make_identity(nc, ident[:])

        for b in range(2):
            eng = nc.vector if b < 4 else nc.gpsimd
            eng.memset(windows[b][:].bitcast(I32), 0)

        nc.vector.tensor_copy(
            wa_codes[:].bitcast(U16).rearrange("p (t m) -> p t m", t=PACK),
            wa_raw[:].bitcast(U16).rearrange("p (m t) -> p t m", t=PACK),
        )
        nc.vector.tensor_copy(
            wa_plane[:].rearrange("p (t m) -> p t m", t=PACK),
            wa_raw_plane[:].rearrange("p (m t) -> p t m", t=PACK),
        )

        wb_codes = keep.tile([P, N], I32, name="wb_codes", tag="raw_words", align_bytes=64)
        nc.sync.dma_start(out=wb_codes[:], in_=wb_words[0].rearrange("p n t -> p (n t)").bitcast(I32))
        ga_rows = keep.tile([P, PACK], F32, name="ga_rows", tag="raw_plane", align_bytes=64)
        nc.sync.dma_start(out=ga_rows[:], in_=ga.rearrange("o (p m) -> p (o m)", m=PACK))

        starts = [sum(CHUNKS[:c]) for c in range(len(CHUNKS))]
        state = {"turn": 0}

        def banks_for(width, per, tags):
            views, groups = [], []
            for g in range(PACK // per):
                bank = psum.tile([P, BANK], F32, name="bank", tag="bank%d" % tags[g])
                v = bank[:, 0 : per * width].rearrange("p (t j) -> p t j", t=per)
                groups.append((v, g * per, per))
                views.extend(v[:, i, :] for i in range(per))
            return views, groups

        def spread_ga(bank_tag):
            views, groups = banks_for(P, PACK, [bank_tag])
            for m in range(PACK):
                nc.tensor.transpose(views[m], ga_rows[:, m : m + 1].to_broadcast([P, P]), ident[:])
            nc.scalar.copy(ga_sb[:].rearrange("p (n m) -> p n m", m=PACK), groups[0][0].rearrange("p m n -> p n m"))

        def late_window(b, tag):
            win = keep.tile([P, T], F32, name="window%d" % b, tag=tag, align_bytes=64)
            nc.gpsimd.memset(win[:].bitcast(I32), 0)
            windows.append(win)

        def gather(c):
            j0, w = starts[c], CHUNKS[c]
            lst = offsets[:, j0 // 16 : (j0 + w) // 16]
            words = keep.tile([P, w], U32, name="xg_words%d" % c, align_bytes=64)
            plane = keep.tile([P, w], U8, name="xg_plane%d" % c, align_bytes=64)
            nc.vector.tensor_copy(words[:], x_words[:].bitcast(U32).indirect(lst))
            nc.vector.tensor_copy(plane[:], x_plane[:].indirect(lst))
            state["x", c] = (words, plane)

        def layer1(c, per_bank, tags):
            j0, w = starts[c], CHUNKS[c]
            words, plane = state["x", c]
            views, groups = banks_for(w, per_bank, tags)
            for v, t0, per in groups:
                for t in range(t0, t0 + per):
                    for s, n in pieces(w):
                        nc.tensor.matmul_mx(
                            out=views[t][:, s : s + n],
                            lhsT=wa_codes[:, 2 * P * t : 2 * P * (t + 1)].bitcast(FP4X4),
                            lhsT_scale=wa_plane[:, P * t : P * (t + 1)],
                            rhs=words[:, s : s + n].bitcast(FP8X4),
                            rhs_scale=plane[:, s : s + n],
                            start=True,
                            stop=True,
                        )
                nc.scalar.activation(h1[t0][:, PAD + j0 : PAD + j0 + w], views[t0], RELU)

        def taps(c):
            j0, w = starts[c], CHUNKS[c]
            hid = keep.tile([P, PACK, w], BF16, name="hid%d" % c, tag="hid1", align_bytes=64)
            for t in range(PACK):
                nc.vector.scalar_tensor_tensor(
                    hid[:, t, :],
                    h1[t][:, PAD + j0 - 1 : PAD + j0 - 1 + w],
                    dc_sb[:, t : t + 1],
                    h1[t][:, PAD + j0 : PAD + j0 + w],
                    MULT,
                    ADD,
                )
            state["hid", c] = hid

        def weave(c, on_vector, tag):
            w = CHUNKS[c]
            grouped = keep.tile([P, w, PACK], BF16, name="grouped%d" % c, tag=tag, align_bytes=64)
            for s, n in pieces(w):
                src = state["hid", c][:, :, s : s + n].rearrange("p t (c i) -> p c t i", i=4)
                dst = grouped[:, s : s + n, :].rearrange("p (c i) t -> p c t i", i=4)
                if on_vector:
                    nc.vector.tensor_copy(dst, src)
                else:
                    nc.scalar.copy(dst, src)
            state["grouped", c] = grouped

        def quantise(c):
            w = CHUNKS[c]
            codes = keep.tile([P, w], U32, name="h_codes%d" % c, tag="h_codes%d" % c, align_bytes=64)
            plane = keep.tile([P, w], U8, name="h_plane%d" % c, align_bytes=64)
            flat = state["grouped", c][:].rearrange("p j t -> p (j t)")
            for s, n in pieces(w):
                nc.vector.quantize_mx(
                    out=codes[:, s : s + n].bitcast(FP8X4),
                    scales=plane[:, s : s + n],
                    in_=flat[:, PACK * s : PACK * (s + n)],
                )
            state["h", c] = (codes, plane)

        def layer2(c, per_bank, tags):
            w = CHUNKS[c]
            codes, plane = state["h", c]
            views, groups = banks_for(w, per_bank, tags)
            state["acc", c] = groups
            for v, b0, per in groups:
                for b in range(b0, b0 + per):
                    for s, n in pieces(w):
                        nc.tensor.matmul_mx(
                            out=views[b][:, s : s + n],
                            lhsT=wb_codes[:, P * b : P * (b + 1)].bitcast(FP8X4),
                            lhsT_scale=wb_plane[:, P * b : P * (b + 1)],
                            rhs=codes[:, s : s + n].bitcast(FP8X4),
                            rhs_scale=plane[:, s : s + n],
                            start=True,
                            stop=True,
                        )

        def drain(c, g, tag):
            v, b0, per = state["acc", c][g]
            p_sb = keep.tile([P, per, CHUNKS[c]], F32, name="p%d_%d" % (c, b0), tag=tag, align_bytes=64)
            nc.scalar.copy(p_sb[:], v)
            for i in range(per):
                state["p", c, b0 + i] = p_sb[:, i, :]

        def scatter(c, blocks):
            j0, w = starts[c], CHUNKS[c]
            lst = offsets[:, j0 // 16 : (j0 + w) // 16]
            for b in blocks:
                nc.vector.tensor_tensor(
                    windows[b][:].indirect(lst), state["p", c, b], ga_sb[:, j0 : j0 + w], MULT
                )
                if c == len(CHUNKS) - 1 and b < 3:
                    nc.sync.dma_start(out=out[P * b : P * (b + 1), :], in_=windows[b][:])
                if c == len(CHUNKS) - 1 and b == 3:
                    half = T // 2
                    nc.sync.dma_start(out=out[P * b : P * (b + 1), 0:half], in_=windows[b][:, 0:half])
                    nc.scalar.dma_start(out=out[P * b : P * (b + 1), half:T], in_=windows[b][:, half:T])

        gather(0)
        layer1(0, 1, [0, 1, 2, 3])
        gather(1)
        taps(0)
        weave(0, True, "grouped0")
        layer1(1, 1, [4, 5, 6, 7])
        spread_ga(2)
        quantise(0)
        late_window(2, "grouped0")
        taps(1)
        late_window(3, "h1_1")
        layer2(0, 2, [0, 1])
        drain(0, 0, "h1_2")
        weave(1, False, "h_codes0")
        drain(0, 1, "hid1")
        scatter(0, [0, 1])
        quantise(1)
        layer2(1, 1, [2, 3, 4, 5])
        for g in range(4):
            drain(1, g, "p1_%d" % g)
        scatter(0, [2, 3])
        scatter(1, range(4))
